import numpy as np
import ml_dtypes


def mxq(x, axis, fmt="e4m3"):
    dtype, down = {"e4m3": (ml_dtypes.float8_e4m3fn, 7), "e5m2": (ml_dtypes.float8_e5m2, 14)}[fmt]
    v = np.moveaxis(np.asarray(x, np.float32).astype(ml_dtypes.bfloat16).astype(np.float64), axis, -1)
    blocks = v.reshape(v.shape[:-1] + (-1, 32))
    amax = np.abs(blocks).max(-1, keepdims=True)
    byte = np.maximum(np.where(amax > 0, np.frexp(amax)[1] - 1 + 127, 0) - down, 1)
    scale = np.exp2(byte - 127.0)
    codes = (blocks / scale).astype(np.float32).astype(dtype).astype(np.float64)
    return np.moveaxis((codes * scale).reshape(v.shape), -1, axis)


WIDE = False


def mx_kscale(k):
    if not WIDE:
        return np.ones(k)
    levels = np.array([10, -10, 5, -5, 0])
    if k % 512:
        return np.exp2(np.random.permutation(np.resize(levels, k // 32))).repeat(32)
    a = np.empty((k // 512, 16))
    for p in range(k // 512):
        a[p, :8] = np.random.permutation(np.resize(levels, 8))
        for g in range(8):
            far = levels[np.abs(levels - a[p, g]) >= 10]
            a[p, g + 8] = far[np.random.randint(len(far))]
    return np.exp2(a.ravel()).repeat(32)


def f64(x):
    return np.asarray(x).astype(np.float64)


def striped(idx):
    return np.tile(idx.reshape(-1, 16).T, (8, 1)).astype(np.uint16)


def unstriped(offs):
    return offs[:16].T.reshape(-1).astype(np.int64)


def striped8(idx):
    return np.concatenate([x.reshape(-1, 16).T for x in idx]).astype(np.uint16)


def runs(offs, k):
    lists = np.stack([offs[16 * r : 16 * r + 16].T.reshape(-1) for r in range(8)]).astype(np.int64)
    return lists[np.arange(k) % 512 // 64]


def pack_weight(w):
    k, n = w.shape
    w = f64(np.asarray(w, np.float32).astype(ml_dtypes.bfloat16)).reshape(k // 32, 32, n)
    amax = np.abs(w).max(1)
    byte = np.clip(np.where(amax > 0, np.frexp(amax)[1] - 1 + 127 - 7, 1), 1, 254)
    scaled = (w * np.exp2(127.0 - byte)[:, None, :]).reshape(k, n).astype(np.float32)
    words = np.ascontiguousarray(scaled.reshape(k // 512, 128, 4, n).transpose(0, 1, 3, 2)).astype(ml_dtypes.float8_e4m3fn).view(np.uint8)
    return words, np.ascontiguousarray(byte.astype(np.uint8).reshape(k // 512, 16, n))


def unpack_weight(words, scales):
    g, p, n, _ = words.shape
    vals = np.ascontiguousarray(words).view(ml_dtypes.float8_e4m3fn).astype(np.float64) * np.repeat(np.exp2(scales.astype(np.float64) - 127.0), 8, axis=1)[..., None]
    return vals.transpose(0, 1, 3, 2).reshape(g * 512, n)


def relu(v):
    return np.maximum(v, 0.0)


K, T, S, V, N, H = 512, 2048, 512, 256, 512, 512


def setup_inputs():
    n = np.random.standard_normal
    s = mx_kscale(K)[:, None]
    u = mx_kscale(H)
    packed_xT = pack_weight(n((K, T)) * s)
    return {
        "x_words": packed_xT[0],
        "x_scales": packed_xT[1],
        "w1": (n((K, H)) / np.sqrt(K) / s).astype(np.float32),
        "gn": (np.random.uniform(0.5, 1.5, (H, 1)) * u[:, None]).astype(np.float32),
        "w2": (n((H, N)) / np.sqrt(H) / u[:, None]).astype(np.float32),
        "offs": striped(np.random.permutation(T)[:S]),
        "n1": striped8(np.stack([np.random.permutation(S) for _ in range(8)])),
        "order": striped8(np.stack([np.random.permutation(S) for _ in range(8)])),
    }


def reference(x_words, x_scales, w1, gn, w2, offs, n1, order):
    xq = unpack_weight(x_words, x_scales)[:, unstriped(offs)]
    y = mxq(f64(w1), 0, "e4m3").T @ xq
    z = f64(gn) * (relu(y) * (relu(y[np.arange(H)[:, None], runs(n1, H)])))
    h = mxq(f64(w2), 0, "e4m3").T @ mxq(z, 0, "e4m3")
    o = h[np.arange(N)[:, None], runs(order, N)]
    mx = o.reshape(N, V, 2).max(axis=2)
    mn = o.reshape(N, V, 2).min(axis=2)
    return mx - mn

@@ -1,0 +1,199 @@
+from contextlib import ExitStack
+
+import concourse.mybir as mybir
+
+F32 = mybir.dt.float32
+BF16 = mybir.dt.bfloat16
+I32 = mybir.dt.int32
+U32 = mybir.dt.uint32
+U16 = mybir.dt.uint16
+U8 = mybir.dt.uint8
+FP8X4 = mybir.dt.float8_e4m3fn_x4
+ALU = mybir.AluOpType
+ACT = mybir.ActivationFunctionType
+
+K, T, S, V, N, H = 512, 2048, 512, 256, 512, 512
+P = 128
+PACK = 4
+HALF = S // 2
+FLOPS = 2 * K * H * S + 2 * H * N * S
+
+
+def tile_picked_corange_none_p_kernel(tc, x_words, x_scales, w1, gn, w2, offs, n1, order, out):
+    nc = tc.nc
+    with ExitStack() as ctx:
+        lists = ctx.enter_context(tc.tile_pool(name="lists", bufs=1))
+        sb = ctx.enter_context(tc.tile_pool(name="sb", bufs=1))
+        ps = ctx.enter_context(tc.psum_pool(name="ps", bufs=1))
+
+        offs_t = lists.tile([P, S // 16], U16, name="offs_t")
+        n1_t = lists.tile([P, S // 16], U16, name="n1_t")
+        order_t = lists.tile([P, S // 16], U16, name="order_t")
+
+        def half_cols(h):
+            return slice(h * HALF, (h + 1) * HALF)
+
+        def half_list(t, h):
+            return t[:, h * HALF // 16:(h + 1) * HALF // 16]
+
+        w1_raw = sb.tile([P, PACK, H], F32, name="w1_raw", tag="w_raw")
+        xw_all = sb.tile([P, T], U32, name="xw_all")
+        xs_all = sb.tile([P, T], U8, name="xs_all")
+        gain = sb.tile([P, PACK], F32, name="gain")
+
+        nc.vector.memset(xs_all[:].bitcast(I32), 0)
+        nc.sync.dma_start(offs_t[:], offs)
+        nc.sync.dma_start(n1_t[:], n1)
+        nc.scalar.dma_start(w1_raw[:], w1.rearrange("(p j) c -> p j c", j=PACK))
+        nc.scalar.dma_start(xw_all[:].bitcast(I32), x_words[0].rearrange("p n t -> p (n t)").bitcast(I32))
+        for q in range(4):
+            nc.sync.dma_start(xs_all[32 * q:32 * q + 4, :].bitcast(I32), x_scales[0, 4 * q:4 * q + 4, :].bitcast(I32))
+        nc.sync.dma_start(gain[:], gn.rearrange("(p t) o -> p (t o)", t=PACK))
+        nc.sync.dma_start(order_t[:], order)
+
+        xs = sb.tile([P, S], U8, name="xs", align_bytes=64)
+        xw = sb.tile([P, S], U32, name="xw", align_bytes=64)
+        nc.vector.tensor_copy(xs[:], xs_all[:].indirect(offs_t[:]))
+
+        def deal(eng, dst, raw, t0, t1, m0, m1):
+            d = dst[:].rearrange("p (t m j) -> p m j t", t=t1 - t0, j=PACK)[:, m0:m1, :, :]
+            s = raw[:].rearrange("p j (m t) -> p m j t", t=PACK)[:, m0:m1, :, t0:t1]
+            if eng == "v":
+                nc.vector.tensor_copy(d, s)
+            else:
+                nc.scalar.copy(d, s)
+
+        w1_b = sb.tile([P, PACK * H], BF16, name="w1_b", align_bytes=64)
+        deal("s", w1_b, w1_raw, 0, 4, 80, 128)
+        deal("v", w1_b, w1_raw, 0, 4, 0, 80)
+        w1_c = sb.tile([P, H], U32, name="w1_c", align_bytes=64)
+        w1_s = sb.tile([P, H], U8, name="w1_s", align_bytes=64)
+        nc.vector.quantize_mx(out=w1_c[:].bitcast(FP8X4), scales=w1_s[:], in_=w1_b[:])
+
+        w2_raw = sb.tile([P, PACK, N], F32, name="w2_raw", tag="w_raw")
+        nc.sync.dma_start(w2_raw[:], w2.rearrange("(p j) c -> p j c", j=PACK))
+
+        for h in range(2):
+            nc.vector.tensor_copy(xw[:, half_cols(h)], xw_all[:].indirect(half_list(offs_t, h)))
+
+        def mm(bank, width, wc, ws, t, rc, rs):
+            acc = ps.tile([P, width], F32, name="acc", tag="bank%d" % bank)
+            nc.tensor.matmul_mx(out=acc[:], lhsT=wc[:, t * P:(t + 1) * P].bitcast(FP8X4), lhsT_scale=ws[:, t * P:(t + 1) * P],
+                                rhs=rc.bitcast(FP8X4), rhs_scale=rs, start=True, stop=True)
+            return acc
+
+        ry = [sb.tile([P, S], F32, name="ry%d" % t) for t in range(4)]
+        gy = [sb.tile([P, S], F32, name="gy%d" % t) for t in range(2)]
+        fy = [sb.tile([P, S], F32, name="fy%d" % t) for t in range(2)]
+        z = [sb.tile([P, PACK, HALF], F32, name="z%d" % h) for h in range(2)]
+        zb = [sb.tile([P, HALF, PACK], BF16, name="zb%d" % h, tag="zb%d" % h, align_bytes=64) for h in range(2)]
+        z_c = sb.tile([P, S], U32, name="z_c", align_bytes=64)
+        z_s = sb.tile([P, S], U8, name="z_s", align_bytes=64)
+
+        for h in range(2):
+            for t in range(2):
+                acc = mm(2 * t + h, HALF, w1_c, w1_s, t, xw[:, half_cols(h)], xs[:, half_cols(h)])
+                nc.scalar.activation(ry[t][:, half_cols(h)], acc[:], ACT.Relu)
+        for t in range(2, 4):
+            acc = mm(2 + t, S, w1_c, w1_s, t, xw[:], xs[:])
+            nc.scalar.activation(ry[t][:], acc[:], ACT.Relu)
+
+        def gained(t, h):
+            nc.vector.tensor_scalar(gy[t][:, half_cols(h)], ry[t][:, half_cols(h)], gain[:, t:t + 1], None, ALU.mult)
+
+        def fused(t, h):
+            nc.vector.tensor_tensor(z[h][:, t, :], ry[t][:].indirect(half_list(n1_t, h)), gy[t][:, half_cols(h)], ALU.mult)
+
+        def fetch(t, h):
+            nc.scalar.activation(fy[t - 2][:, half_cols(h)], ry[t][:].indirect(half_list(n1_t, h)), ACT.Copy)
+
+        def product(t, h):
+            nc.vector.scalar_tensor_tensor(z[h][:, t, :], ry[t][:, half_cols(h)], gain[:, t:t + 1], fy[t - 2][:, half_cols(h)], ALU.mult, ALU.mult)
+
+        def weave(h):
+            nc.vector.tensor_copy(zb[h][:].rearrange("p (c i) t -> p c t i", i=4), z[h][:].rearrange("p t (c i) -> p c t i", i=4))
+
+        def quant_z(h):
+            nc.vector.quantize_mx(out=z_c[:, half_cols(h)].bitcast(FP8X4), scales=z_s[:, half_cols(h)],
+                                  in_=zb[h][:].rearrange("p c t -> p (c t)"))
+
+        w2_b = [sb.tile([P, 2 * N], BF16, name="w2_b0", align_bytes=64)]
+        w2_c = sb.tile([P, N], U32, name="w2_c", align_bytes=64)
+        w2_s = sb.tile([P, N], U8, name="w2_s", align_bytes=64)
+
+        def quant_w2(u):
+            nc.vector.quantize_mx(out=w2_c[:, 256 * u:256 * (u + 1)].bitcast(FP8X4), scales=w2_s[:, 256 * u:256 * (u + 1)], in_=w2_b[u][:])
+
+        gained(0, 0)
+        gained(1, 0)
+        fused(0, 0)
+        fused(1, 0)
+        fetch(2, 0)
+        fetch(3, 0)
+        gained(0, 1)
+        gained(1, 1)
+        fused(0, 1)
+        fused(1, 1)
+        fetch(2, 1)
+        fetch(3, 1)
+        deal("s", w2_b[0], w2_raw, 0, 2, 0, 128)
+        product(2, 0)
+        product(3, 0)
+        weave(0)
+        product(2, 1)
+        quant_z(0)
+        product(3, 1)
+        weave(1)
+        quant_w2(0)
+        quant_z(1)
+        w2_b.append(sb.tile([P, 2 * N], BF16, name="w2_b1", tag="zb1", align_bytes=64))
+        deal("v", w2_b[1], w2_raw, 2, 4, 0, 128)
+        quant_w2(1)
+
+        hh = [sb.tile([P, S], F32, name="hh%d" % t) for t in range(4)]
+        oo = [sb.tile([P, S], F32, name="oo%d" % t) for t in range(4)]
+        dd = [sb.tile([P, V], F32, name="dd%d" % t) for t in range(4)]
+        rr = [sb.tile([P, V], F32, name="rr%d" % t) for t in range(4)]
+        for h in range(2):
+            for t in range(2):
+                acc = mm(2 * t + h, HALF, w2_c, w2_s, t, z_c[:, half_cols(h)], z_s[:, half_cols(h)])
+                nc.scalar.copy(hh[t][:, half_cols(h)], acc[:])
+        for t in range(2, 4):
+            acc = mm(2 + t, S, w2_c, w2_s, t, z_c[:], z_s[:])
+            nc.scalar.copy(hh[t][:], acc[:])
+
+        out_v = out.rearrange("(p t) v -> p t v", t=PACK)
+
+        def line_up(eng, t, h):
+            src = hh[t][:].indirect(half_list(order_t, h))
+            if eng == "v":
+                nc.vector.tensor_copy(oo[t][:, half_cols(h)], src)
+            else:
+                nc.scalar.activation(oo[t][:, half_cols(h)], src, ACT.Copy)
+
+        def diff(t):
+            nc.vector.tensor_tensor(dd[t][:], oo[t][:, 0:S:2], oo[t][:, 1:S:2], ALU.subtract)
+
+        def finish(eng, t):
+            if eng == "v":
+                nc.vector.scalar_tensor_tensor(rr[t][:], dd[t][:], -1.0, dd[t][:], ALU.mult, ALU.max)
+            else:
+                nc.scalar.activation(rr[t][:], dd[t][:], ACT.Abs)
+            nc.sync.dma_start(out_v[:, t, :], rr[t][:])
+
+        line_up("v", 0, 0)
+        line_up("v", 0, 1)
+        line_up("s", 1, 0)
+        line_up("v", 1, 1)
+        line_up("s", 2, 0)
+        line_up("s", 2, 1)
+        diff(0)
+        diff(1)
+        finish("v", 0)
+        finish("v", 1)
+        line_up("s", 3, 0)
+        line_up("v", 3, 1)
+        diff(2)
+        diff(3)
+        finish("s", 2)
+        finish("s", 3)

@@ -41,15 +41,16 @@ def tile_picked_corange_none_p_kernel(tc, x_words, x_scales, w1, gn, w2, offs, n
         xs_all = sb.tile([P, T], U8, name="xs_all")
         gain = sb.tile([P, PACK], F32, name="gain")
 
-        nc.vector.memset(xs_all[:].bitcast(I32), 0)
+        nc.gpsimd.memset(xs_all[:, :1280].bitcast(I32), 0)
+        nc.vector.memset(xs_all[:, 1280:].bitcast(I32), 0)
         nc.sync.dma_start(offs_t[:], offs)
+        nc.sync.dma_start(w1_raw[:], w1.rearrange("(p j) c -> p j c", j=PACK))
         nc.sync.dma_start(n1_t[:], n1)
-        nc.scalar.dma_start(w1_raw[:], w1.rearrange("(p j) c -> p j c", j=PACK))
-        nc.scalar.dma_start(xw_all[:].bitcast(I32), x_words[0].rearrange("p n t -> p (n t)").bitcast(I32))
+        nc.sync.dma_start(order_t[:], order)
         for q in range(4):
             nc.sync.dma_start(xs_all[32 * q:32 * q + 4, :].bitcast(I32), x_scales[0, 4 * q:4 * q + 4, :].bitcast(I32))
-        nc.sync.dma_start(gain[:], gn.rearrange("(p t) o -> p (t o)", t=PACK))
-        nc.sync.dma_start(order_t[:], order)
+        nc.sync.dma_start(xw_all[:].bitcast(I32), x_words[0].rearrange("p n t -> p (n t)").bitcast(I32))
+        nc.gpsimd.dma_start(gain[:], gn.rearrange("(p t) o -> p (t o)", t=PACK))
 
         xs = sb.tile([P, S], U8, name="xs", align_bytes=64)
         xw = sb.tile([P, S], U32, name="xw", align_bytes=64)
@@ -70,11 +71,11 @@ def tile_picked_corange_none_p_kernel(tc, x_words, x_scales, w1, gn, w2, offs, n
         w1_s = sb.tile([P, H], U8, name="w1_s", align_bytes=64)
         nc.vector.quantize_mx(out=w1_c[:].bitcast(FP8X4), scales=w1_s[:], in_=w1_b[:])
 
-        w2_raw = sb.tile([P, PACK, N], F32, name="w2_raw", tag="w_raw")
-        nc.sync.dma_start(w2_raw[:], w2.rearrange("(p j) c -> p j c", j=PACK))
-
         for h in range(2):
             nc.vector.tensor_copy(xw[:, half_cols(h)], xw_all[:].indirect(half_list(offs_t, h)))
+
+        w2_raw = sb.tile([P, PACK, N], F32, name="w2_raw", tag="w_raw")
+        nc.sync.dma_start(w2_raw[:], w2.rearrange("(p j) c -> p j c", j=PACK))
 
         def mm(bank, width, wc, ws, t, rc, rs):
             acc = ps.tile([P, width], F32, name="acc", tag="bank%d" % bank)
@@ -83,7 +84,7 @@ def tile_picked_corange_none_p_kernel(tc, x_words, x_scales, w1, gn, w2, offs, n
             return acc
 
         ry = [sb.tile([P, S], F32, name="ry%d" % t) for t in range(4)]
-        gy = [sb.tile([P, S], F32, name="gy%d" % t) for t in range(2)]
+        gy = [sb.tile([P, S], F32, name="gy%d" % t, tag="gy%d" % t, align_bytes=64) for t in range(2)]
         fy = [sb.tile([P, S], F32, name="fy%d" % t) for t in range(2)]
         z = [sb.tile([P, PACK, HALF], F32, name="z%d" % h) for h in range(2)]
         zb = [sb.tile([P, HALF, PACK], BF16, name="zb%d" % h, tag="zb%d" % h, align_bytes=64) for h in range(2)]
@@ -110,14 +111,19 @@ def tile_picked_corange_none_p_kernel(tc, x_words, x_scales, w1, gn, w2, offs, n
         def product(t, h):
             nc.vector.scalar_tensor_tensor(z[h][:, t, :], ry[t][:, half_cols(h)], gain[:, t:t + 1], fy[t - 2][:, half_cols(h)], ALU.mult, ALU.mult)
 
-        def weave(h):
-            nc.vector.tensor_copy(zb[h][:].rearrange("p (c i) t -> p c t i", i=4), z[h][:].rearrange("p t (c i) -> p c t i", i=4))
+        def weave(eng, h, a, b):
+            d = zb[h][:, a:b, :].rearrange("p (c i) t -> p c t i", i=4)
+            s = z[h][:, :, a:b].rearrange("p t (c i) -> p c t i", i=4)
+            if eng == "v":
+                nc.vector.tensor_copy(d, s)
+            else:
+                nc.scalar.copy(d, s)
 
         def quant_z(h):
             nc.vector.quantize_mx(out=z_c[:, half_cols(h)].bitcast(FP8X4), scales=z_s[:, half_cols(h)],
                                   in_=zb[h][:].rearrange("p c t -> p (c t)"))
 
-        w2_b = [sb.tile([P, 2 * N], BF16, name="w2_b0", align_bytes=64)]
+        w2_b = []
         w2_c = sb.tile([P, N], U32, name="w2_c", align_bytes=64)
         w2_s = sb.tile([P, N], U8, name="w2_s", align_bytes=64)
 
@@ -136,18 +142,20 @@ def tile_picked_corange_none_p_kernel(tc, x_words, x_scales, w1, gn, w2, offs, n
         fused(1, 1)
         fetch(2, 1)
         fetch(3, 1)
+        w2_b.append(sb.tile([P, 2 * N], BF16, name="w2_b0", tag="gy1", align_bytes=64))
         deal("s", w2_b[0], w2_raw, 0, 2, 0, 128)
         product(2, 0)
         product(3, 0)
-        weave(0)
+        weave("v", 0, 0, HALF)
         product(2, 1)
-        quant_z(0)
         product(3, 1)
-        weave(1)
+        quant_z(0)
+        weave("v", 1, 0, 160)
+        weave("s", 1, 160, HALF)
         quant_w2(0)
         quant_z(1)
-        w2_b.append(sb.tile([P, 2 * N], BF16, name="w2_b1", tag="zb1", align_bytes=64))
-        deal("v", w2_b[1], w2_raw, 2, 4, 0, 128)
+        w2_b.append(sb.tile([P, 2 * N], BF16, name="w2_b1", tag="zb0", align_bytes=64))
+        deal("s", w2_b[1], w2_raw, 2, 4, 0, 128)
         quant_w2(1)
 
         hh = [sb.tile([P, S], F32, name="hh%d" % t) for t in range(4)]
@@ -157,7 +165,10 @@ def tile_picked_corange_none_p_kernel(tc, x_words, x_scales, w1, gn, w2, offs, n
         for h in range(2):
             for t in range(2):
                 acc = mm(2 * t + h, HALF, w2_c, w2_s, t, z_c[:, half_cols(h)], z_s[:, half_cols(h)])
-                nc.scalar.copy(hh[t][:, half_cols(h)], acc[:])
+                if (t, h) == (0, 1):
+                    nc.vector.tensor_copy(hh[t][:, half_cols(h)], acc[:])
+                else:
+                    nc.scalar.copy(hh[t][:, half_cols(h)], acc[:])
         for t in range(2, 4):
             acc = mm(2 + t, S, w2_c, w2_s, t, z_c[:], z_s[:])
             nc.scalar.copy(hh[t][:], acc[:])
@@ -171,29 +182,31 @@ def tile_picked_corange_none_p_kernel(tc, x_words, x_scales, w1, gn, w2, offs, n
             else:
                 nc.scalar.activation(oo[t][:, half_cols(h)], src, ACT.Copy)
 
-        def diff(t):
-            nc.vector.tensor_tensor(dd[t][:], oo[t][:, 0:S:2], oo[t][:, 1:S:2], ALU.subtract)
+        def diff(t, a, b):
+            nc.vector.tensor_tensor(dd[t][:, a:b], oo[t][:, 2 * a:2 * b:2], oo[t][:, 2 * a + 1:2 * b:2], ALU.subtract)
 
-        def finish(eng, t):
+        def finish(eng, t, a, b):
             if eng == "v":
-                nc.vector.scalar_tensor_tensor(rr[t][:], dd[t][:], -1.0, dd[t][:], ALU.mult, ALU.max)
+                nc.vector.scalar_tensor_tensor(rr[t][:, a:b], dd[t][:, a:b], -1.0, dd[t][:, a:b], ALU.mult, ALU.max)
             else:
-                nc.scalar.activation(rr[t][:], dd[t][:], ACT.Abs)
-            nc.sync.dma_start(out_v[:, t, :], rr[t][:])
+                nc.scalar.activation(rr[t][:, a:b], dd[t][:, a:b], ACT.Abs)
+            nc.sync.dma_start(out_v[:, t, a:b], rr[t][:, a:b])
 
         line_up("v", 0, 0)
         line_up("v", 0, 1)
         line_up("s", 1, 0)
         line_up("v", 1, 1)
+        diff(0, 0, V)
         line_up("s", 2, 0)
-        line_up("s", 2, 1)
-        diff(0)
-        diff(1)
-        finish("v", 0)
-        finish("v", 1)
+        diff(1, 0, V)
+        line_up("v", 2, 1)
+        finish("v", 0, 0, V)
         line_up("s", 3, 0)
-        line_up("v", 3, 1)
-        diff(2)
-        diff(3)
-        finish("s", 2)
-        finish("s", 3)
+        line_up("s", 3, 1)
+        finish("v", 1, 0, V)
+        diff(2, 0, V)
+        diff(3, 0, V // 2)
+        diff(3, V // 2, V)
+        finish("s", 2, 0, V)
+        finish("s", 3, 0, V // 2)
+        finish("v", 3, V // 2, V)

from contextlib import ExitStack

import concourse.mybir as mybir

F32 = mybir.dt.float32
BF16 = mybir.dt.bfloat16
I32 = mybir.dt.int32
U32 = mybir.dt.uint32
U16 = mybir.dt.uint16
U8 = mybir.dt.uint8
FP8X4 = mybir.dt.float8_e4m3fn_x4
ALU = mybir.AluOpType
ACT = mybir.ActivationFunctionType

K, T, S, V, N, H = 512, 2048, 512, 256, 512, 512
P = 128
PACK = 4
HALF = S // 2
FLOPS = 2 * K * H * S + 2 * H * N * S


def tile_picked_corange_none_p_kernel(tc, x_words, x_scales, w1, gn, w2, offs, n1, order, out):
    nc = tc.nc
    with ExitStack() as ctx:
        lists = ctx.enter_context(tc.tile_pool(name="lists", bufs=1))
        sb = ctx.enter_context(tc.tile_pool(name="sb", bufs=1))
        ps = ctx.enter_context(tc.psum_pool(name="ps", bufs=1))

        offs_t = lists.tile([P, S // 16], U16, name="offs_t")
        n1_t = lists.tile([P, S // 16], U16, name="n1_t")
        order_t = lists.tile([P, S // 16], U16, name="order_t")

        def half_cols(h):
            return slice(h * HALF, (h + 1) * HALF)

        def half_list(t, h):
            return t[:, h * HALF // 16:(h + 1) * HALF // 16]

        w1_raw = sb.tile([P, PACK, H], F32, name="w1_raw", tag="w_raw")
        xw_all = sb.tile([P, T], U32, name="xw_all")
        xs_all = sb.tile([P, T], U8, name="xs_all")
        gain = sb.tile([P, PACK], F32, name="gain")

        nc.gpsimd.memset(xs_all[:, :1280].bitcast(I32), 0)
        nc.vector.memset(xs_all[:, 1280:].bitcast(I32), 0)
        nc.sync.dma_start(offs_t[:], offs)
        nc.sync.dma_start(w1_raw[:], w1.rearrange("(p j) c -> p j c", j=PACK))
        nc.sync.dma_start(n1_t[:], n1)
        nc.sync.dma_start(order_t[:], order)
        for q in range(4):
            nc.sync.dma_start(xs_all[32 * q:32 * q + 4, :].bitcast(I32), x_scales[0, 4 * q:4 * q + 4, :].bitcast(I32))
        nc.sync.dma_start(xw_all[:].bitcast(I32), x_words[0].rearrange("p n t -> p (n t)").bitcast(I32))
        nc.gpsimd.dma_start(gain[:], gn.rearrange("(p t) o -> p (t o)", t=PACK))

        xs = sb.tile([P, S], U8, name="xs", align_bytes=64)
        xw = sb.tile([P, S], U32, name="xw", align_bytes=64)
        nc.vector.tensor_copy(xs[:], xs_all[:].indirect(offs_t[:]))

        def deal(eng, dst, raw, t0, t1, m0, m1):
            d = dst[:].rearrange("p (t m j) -> p m j t", t=t1 - t0, j=PACK)[:, m0:m1, :, :]
            s = raw[:].rearrange("p j (m t) -> p m j t", t=PACK)[:, m0:m1, :, t0:t1]
            if eng == "v":
                nc.vector.tensor_copy(d, s)
            else:
                nc.scalar.copy(d, s)

        w1_b = sb.tile([P, PACK * H], BF16, name="w1_b", align_bytes=64)
        deal("s", w1_b, w1_raw, 0, 4, 80, 128)
        deal("v", w1_b, w1_raw, 0, 4, 0, 80)
        w1_c = sb.tile([P, H], U32, name="w1_c", align_bytes=64)
        w1_s = sb.tile([P, H], U8, name="w1_s", align_bytes=64)
        nc.vector.quantize_mx(out=w1_c[:].bitcast(FP8X4), scales=w1_s[:], in_=w1_b[:])

        for h in range(2):
            nc.vector.tensor_copy(xw[:, half_cols(h)], xw_all[:].indirect(half_list(offs_t, h)))

        w2_raw = sb.tile([P, PACK, N], F32, name="w2_raw", tag="w_raw")
        nc.sync.dma_start(w2_raw[:], w2.rearrange("(p j) c -> p j c", j=PACK))

        def mm(bank, width, wc, ws, t, rc, rs):
            acc = ps.tile([P, width], F32, name="acc", tag="bank%d" % bank)
            nc.tensor.matmul_mx(out=acc[:], lhsT=wc[:, t * P:(t + 1) * P].bitcast(FP8X4), lhsT_scale=ws[:, t * P:(t + 1) * P],
                                rhs=rc.bitcast(FP8X4), rhs_scale=rs, start=True, stop=True)
            return acc

        ry = [sb.tile([P, S], F32, name="ry%d" % t) for t in range(4)]
        gy = [sb.tile([P, S], F32, name="gy%d" % t, tag="gy%d" % t, align_bytes=64) for t in range(2)]
        fy = [sb.tile([P, S], F32, name="fy%d" % t) for t in range(2)]
        z = [sb.tile([P, PACK, HALF], F32, name="z%d" % h) for h in range(2)]
        zb = [sb.tile([P, HALF, PACK], BF16, name="zb%d" % h, tag="zb%d" % h, align_bytes=64) for h in range(2)]
        z_c = sb.tile([P, S], U32, name="z_c", align_bytes=64)
        z_s = sb.tile([P, S], U8, name="z_s", align_bytes=64)

        for h in range(2):
            for t in range(2):
                acc = mm(2 * t + h, HALF, w1_c, w1_s, t, xw[:, half_cols(h)], xs[:, half_cols(h)])
                nc.scalar.activation(ry[t][:, half_cols(h)], acc[:], ACT.Relu)
        for t in range(2, 4):
            acc = mm(2 + t, S, w1_c, w1_s, t, xw[:], xs[:])
            nc.scalar.activation(ry[t][:], acc[:], ACT.Relu)

        def gained(t, h):
            nc.vector.tensor_scalar(gy[t][:, half_cols(h)], ry[t][:, half_cols(h)], gain[:, t:t + 1], None, ALU.mult)

        def fused(t, h):
            nc.vector.tensor_tensor(z[h][:, t, :], ry[t][:].indirect(half_list(n1_t, h)), gy[t][:, half_cols(h)], ALU.mult)

        def fetch(t, h):
            nc.scalar.activation(fy[t - 2][:, half_cols(h)], ry[t][:].indirect(half_list(n1_t, h)), ACT.Copy)

        def product(t, h):
            nc.vector.scalar_tensor_tensor(z[h][:, t, :], ry[t][:, half_cols(h)], gain[:, t:t + 1], fy[t - 2][:, half_cols(h)], ALU.mult, ALU.mult)

        def weave(eng, h, a, b):
            d = zb[h][:, a:b, :].rearrange("p (c i) t -> p c t i", i=4)
            s = z[h][:, :, a:b].rearrange("p t (c i) -> p c t i", i=4)
            if eng == "v":
                nc.vector.tensor_copy(d, s)
            else:
                nc.scalar.copy(d, s)

        def quant_z(h):
            nc.vector.quantize_mx(out=z_c[:, half_cols(h)].bitcast(FP8X4), scales=z_s[:, half_cols(h)],
                                  in_=zb[h][:].rearrange("p c t -> p (c t)"))

        w2_b = []
        w2_c = sb.tile([P, N], U32, name="w2_c", align_bytes=64)
        w2_s = sb.tile([P, N], U8, name="w2_s", align_bytes=64)

        def quant_w2(u):
            nc.vector.quantize_mx(out=w2_c[:, 256 * u:256 * (u + 1)].bitcast(FP8X4), scales=w2_s[:, 256 * u:256 * (u + 1)], in_=w2_b[u][:])

        gained(0, 0)
        gained(1, 0)
        fused(0, 0)
        fused(1, 0)
        fetch(2, 0)
        fetch(3, 0)
        gained(0, 1)
        gained(1, 1)
        fused(0, 1)
        fused(1, 1)
        fetch(2, 1)
        fetch(3, 1)
        w2_b.append(sb.tile([P, 2 * N], BF16, name="w2_b0", tag="gy1", align_bytes=64))
        deal("s", w2_b[0], w2_raw, 0, 2, 0, 128)
        product(2, 0)
        product(3, 0)
        weave("v", 0, 0, HALF)
        product(2, 1)
        product(3, 1)
        quant_z(0)
        weave("v", 1, 0, 160)
        weave("s", 1, 160, HALF)
        quant_w2(0)
        quant_z(1)
        w2_b.append(sb.tile([P, 2 * N], BF16, name="w2_b1", tag="zb0", align_bytes=64))
        deal("s", w2_b[1], w2_raw, 2, 4, 0, 128)
        quant_w2(1)

        hh = [sb.tile([P, S], F32, name="hh%d" % t) for t in range(4)]
        oo = [sb.tile([P, S], F32, name="oo%d" % t) for t in range(4)]
        dd = [sb.tile([P, V], F32, name="dd%d" % t) for t in range(4)]
        rr = [sb.tile([P, V], F32, name="rr%d" % t) for t in range(4)]
        for h in range(2):
            for t in range(2):
                acc = mm(2 * t + h, HALF, w2_c, w2_s, t, z_c[:, half_cols(h)], z_s[:, half_cols(h)])
                if (t, h) == (0, 1):
                    nc.vector.tensor_copy(hh[t][:, half_cols(h)], acc[:])
                else:
                    nc.scalar.copy(hh[t][:, half_cols(h)], acc[:])
        for t in range(2, 4):
            acc = mm(2 + t, S, w2_c, w2_s, t, z_c[:], z_s[:])
            nc.scalar.copy(hh[t][:], acc[:])

        out_v = out.rearrange("(p t) v -> p t v", t=PACK)

        def line_up(eng, t, h):
            src = hh[t][:].indirect(half_list(order_t, h))
            if eng == "v":
                nc.vector.tensor_copy(oo[t][:, half_cols(h)], src)
            else:
                nc.scalar.activation(oo[t][:, half_cols(h)], src, ACT.Copy)

        def diff(t, a, b):
            nc.vector.tensor_tensor(dd[t][:, a:b], oo[t][:, 2 * a:2 * b:2], oo[t][:, 2 * a + 1:2 * b:2], ALU.subtract)

        def finish(eng, t, a, b):
            if eng == "v":
                nc.vector.scalar_tensor_tensor(rr[t][:, a:b], dd[t][:, a:b], -1.0, dd[t][:, a:b], ALU.mult, ALU.max)
            else:
                nc.scalar.activation(rr[t][:, a:b], dd[t][:, a:b], ACT.Abs)
            nc.sync.dma_start(out_v[:, t, a:b], rr[t][:, a:b])

        line_up("v", 0, 0)
        line_up("v", 0, 1)
        line_up("s", 1, 0)
        line_up("v", 1, 1)
        diff(0, 0, V)
        line_up("s", 2, 0)
        diff(1, 0, V)
        line_up("v", 2, 1)
        finish("v", 0, 0, V)
        line_up("s", 3, 0)
        line_up("s", 3, 1)
        finish("v", 1, 0, V)
        diff(2, 0, V)
        diff(3, 0, V // 2)
        diff(3, V // 2, V)
        finish("s", 2, 0, V)
        finish("s", 3, 0, V // 2)
        finish("v", 3, V // 2, V)
